import numpy as np, ml_dtypes
CORES = [65,73,81,89,97,105,113,121]
N = 8
R, TK = 16, 512
WID = [192,192,512,64,384,128,64,128]
def setup_inputs(rng):
    u = (rng.standard_normal((N, 128, R), dtype=np.float32) / 11).astype(ml_dtypes.bfloat16)
    return {"x": rng.standard_normal((N, 128, TK), dtype=np.float32).astype(ml_dtypes.bfloat16), "u": u, "ut": u.transpose(0, 2, 1).copy(), "vt": rng.standard_normal((N, R, 128), dtype=np.float32).astype(ml_dtypes.bfloat16)}
def setup_inputs_big(rng):
    d = setup_inputs(rng)
    for k in ("x", "u", "ut", "vt"): d[k] = (d[k].astype(np.float32) * 1024.0).astype(d[k].dtype)
    return d
def setup_inputs_small(rng):
    d = setup_inputs(rng)
    for k in ("x", "u", "ut", "vt"): d[k] = (d[k].astype(np.float32) * (1 / 1024.0)).astype(d[k].dtype)
    return d
def setup_inputs_apart(rng):
    d = setup_inputs(rng)
    f = (10.0 ** rng.permutation(np.linspace(-1.5, 1.5, N))).astype(np.float32).reshape(N, 1, 1)
    for k in ("x", "u", "ut", "vt"): d[k] = (d[k].astype(np.float32) * f).astype(d[k].dtype)
    return d
def whole(x, u, ut, vt):
    X, U, VT = x.astype(np.float64), u.astype(np.float64), vt.astype(np.float64)
    y = np.stack([sum(VT[j].T @ (U[j].T @ X[r]) for j in range(N)) for r in range(N)])
    return {"y": y.astype(ml_dtypes.bfloat16)}
def reference(x, u, ut, vt):
    o = whole(x, u, ut, vt)["y"].copy()
    for r in range(N):
        o[r][:, WID[r]:] = np.nan
    return {"y": o}

from concourse.bass import DstId, RemoteDMATransfer

SCRATCH = {
    "D": ("dram", [8, 128, 32], "bfloat16"),
    "H": ("dram", [128, 32], "bfloat16"),
    "FU": ("sbuf", [128, 128], "bfloat16"),
    "FV": ("sbuf", [128, 128], "bfloat16"),
    "X": ("sbuf", [128, 512], "bfloat16"),
    "WTs": ("sbuf", [128, 128], "bfloat16"),
    "Ys": ("sbuf", [128, 512], "bfloat16"),
    "WTp": ("psum", [128, 512], "float32"),
    "Yp0": ("psum", [128, 512], "float32"),
    "Yp1": ("psum", [128, 512], "float32"),
}
SEMAPHORES = ["ld", "xl", "sent", "hin", "near", "far", "fn", "ff", "wa", "wt", "wc", "y0", "y1", "yc", "st"]

HELPERS = 2


def _lanes(topo, src, dst):
    m = topo.mask(src, dst)
    return [b for b in range(m.bit_length()) if (m >> b) & 1][0::2]


def _plan(T, topo):
    cores = list(T.cores)
    n = len(cores)
    chips = [topo.chip(c) for c in cores]
    a = [j for j in range(n) if chips[j] == chips[0] or topo.same_plane(chips[j], chips[0])]
    b = [j for j in range(n) if j not in a]
    order = a + b
    plan = {}
    for j in range(n):
        mine, other = (a, b) if j in a else (b, a)
        hs = [k for k in range(topo.CHIPS * topo.CORES_PER_CHIP)
              if topo.chip(k) == chips[j] and k not in cores
              and all(topo.may_write(k, cores[i]) for i in other)]
        hs.sort(key=lambda k: (topo.die(k) != topo.die(cores[j]), k))
        hs = hs[:HELPERS]
        plan[j] = {
            "pos": order.index(j),
            "block": 0 if j in a else 1,
            "near": [i for i in mine if i != j],
            "helpers": [(h, other[t::len(hs)]) for t, h in enumerate(hs)],
            "nfar": len(other),
        }
    return plan, len(a)


def _xfer(topo, src_core, dst_core, lane, sem, src, dst):
    rid, pid, _ = topo.addr(dst_core)
    return RemoteDMATransfer(dst_ids=[DstId(rid=rid, pnc=pid)],
                             dma_engine_mask=1 << _lanes(topo, src_core, dst_core)[lane],
                             remote_sem=sem, src=src, dst=dst)


def rank_program(g, core, T, topo):
    s = T.sem
    cores = list(T.cores)
    plan, half = _plan(T, topo)
    rank = T.rank_of(core)

    if rank is None:
        for j, pl in plan.items():
            for h, dsts in pl["helpers"]:
                if h == core:
                    g.wait_ge(s.hin, 1)
                    g.remote_dma_fused(
                        [_xfer(topo, core, cores[i], t, s.far, T.H[:, :], T.D[pl["pos"]])
                         for t, i in enumerate(dsts)], local_sem=s.sent)
                    g.wait_ge(s.sent, len(dsts))
        return

    pl = plan[rank]
    pos = pl["pos"]
    W = T.tables["WID"][rank]
    rows = 128 // (2 * half) * half
    nb, fb = pl["block"], 1 - pl["block"]

    g.sync.dma_start(T.D[pos, 0:64, :], T.ut[:, :]).then_inc(s.ld, 16)
    g.scalar.dma_start(T.D[pos, 64:128, :], T.vt[:, :]).then_inc(s.ld, 16)
    g.sync.dma_start(T.X[:, 0:W], T.x[:, 0:W]).then_inc(s.xl, 16)

    g.wait_ge(s.ld, 32)
    g.remote_dma_fused([_xfer(topo, core, h, t, s.hin, T.D[pos], T.H[:, :])
                        for t, (h, _) in enumerate(pl["helpers"])], local_sem=s.sent)
    g.remote_dma_fused([_xfer(topo, core, cores[i], t, s.near, T.D[pos], T.D[pos])
                        for t, i in enumerate(pl["near"])], local_sem=s.sent)

    for q, buf, lo in ((g.sync, T.FU, 0), (g.scalar, T.FV, 64)):
        q.wait_ge(s.ld, 32)
        q.wait_ge(s.near, len(pl["near"]))
        q.dma_start(buf[nb * rows:(nb + 1) * rows, :],
                    T.D[nb * half:(nb + 1) * half, lo:lo + 64, :]).then_inc(s.fn, 16)
        q.wait_ge(s.far, pl["nfar"])
        q.dma_start(buf[fb * rows:(fb + 1) * rows, :],
                    T.D[fb * half:(fb + 1) * half, lo:lo + 64, :]).then_inc(s.ff, 16)

    g.tensor.wait_ge(s.fn, 32)
    g.tensor.matmul(T.WTp[:, 0:128], T.FU[nb * rows:(nb + 1) * rows, :], T.FV[nb * rows:(nb + 1) * rows, :],
                    True, False).then_inc(s.wa, 1)
    g.tensor.wait_ge(s.wa, 1)
    g.tensor.wait_ge(s.ff, 32)
    g.tensor.matmul(T.WTp[:, 0:128], T.FU[fb * rows:(fb + 1) * rows, :], T.FV[fb * rows:(fb + 1) * rows, :],
                    False, True).then_inc(s.wt, 1)
    g.vector.wait_ge(s.wt, 1)
    g.vector.tensor_copy(T.WTs[:, :], T.WTp[:, 0:128]).then_inc(s.wc, 1)

    cuts = [0, W] if W <= 128 else [0, W // 2, W]
    g.tensor.wait_ge(s.xl, 16)
    g.tensor.wait_ge(s.wc, 1)
    for i in range(len(cuts) - 1):
        c0, c1 = cuts[i], cuts[i + 1]
        yp = T["Yp%d" % i]
        ys = s["y%d" % i]
        g.tensor.matmul(yp[:, 0:c1 - c0], T.WTs[:, :], T.X[:, c0:c1], True, True).then_inc(ys, 1)
        g.vector.wait_ge(ys, 1)
        g.vector.tensor_copy(T.Ys[:, c0:c1], yp[:, 0:c1 - c0]).then_inc(s.yc, 1)
    g.sync.wait_ge(s.yc, len(cuts) - 1)
    g.sync.dma_start(T.y[:, 0:W], T.Ys[:, 0:W]).then_inc(s.st, 16)
    g.sync.wait_ge(s.st, 16)
    g.wait_ge(s.sent, len(pl["helpers"]) + len(pl["near"]))
